import numpy as np, ml_dtypes
CORES = [16,17,18,19,20,21,22,23,32,33,34,35,36,37,38,39,48,49,50,51,52,53,54,55]
N = 24
G1 = [0,8,16]
G2 = [0,1,2,3,4,5,6,7,8,9,10,11,12,13,14,15,16,17,18,19,20,21,22,23]
def setup_inputs(rng):
    return {"x1": rng.standard_normal((N, 128, 256), dtype=np.float32).astype(ml_dtypes.bfloat16), "x2": rng.standard_normal((N, 128, 504), dtype=np.float32)}
def reference(x1, x2):
    out = {}
    y = np.full((N, 128, 768), np.nan, x1.dtype)
    s = np.concatenate([x1[r] for r in G1], axis=1)
    for r in G1:
        y[r] = s
    out["y1"] = y
    y = np.full((N, 128, 21), np.nan, x2.dtype)
    s = x2[G2].sum(axis=0, dtype=np.float64).astype(x2.dtype)
    for i, r in enumerate(G2):
        y[r] = s[:, 21 * i:21 * i + 21]
    out["y2"] = y
    return out

@@ -1,0 +1,119 @@
+from concourse.bass import DstId, RemoteDMATransfer
+
+SCRATCH = {
+    "d": ("dram", [12, 128, 42], "float32"),
+    "r1": ("dram", [8, 128, 42], "float32"),
+    "r2": ("dram", [8, 128, 42], "float32"),
+    "pr": ("dram", [3, 128, 42], "float32"),
+    "fin": ("dram", [2, 128, 42], "float32"),
+    "a1": ("dram", [128, 256], "bfloat16"),
+    "agl": ("dram", [3, 128, 256], "bfloat16"),
+}
+SEMAPHORES = ["ld1", "ld2", "e1", "e2", "f1", "f2", "snd", "st", "agld", "aga"]
+
+
+def _piece(c, h, q2):
+    return (c * 2 + h) * 2 + q2
+
+
+def _finisher(h, q2):
+    return 4 * (1 - h) + 2 + q2
+
+
+def rank_program(g, core, T, topo):
+    rank = T.rank_of(core)
+    if rank is None:
+        return
+    S = T.sem
+    ci, k = divmod(rank, 8)
+    others = [c for c in range(3) if c != ci]
+    G1 = T.tables["G1"]
+    in_ag = rank in G1
+
+    def did(c, kk):
+        rid, pid, _se = topo.addr(T.cores[8 * c + kk])
+        return DstId(rid=rid, pnc=pid)
+
+    def role(kk):
+        return others[(kk % 4) // 2], 1 - kk // 4, kk % 2
+
+    def load(q, c, h, sem):
+        p = _piece(c, h, 0)
+        col = 168 * c + 84 * h
+        q.dma_start(T.d[p:p + 2], T.x2[:, col:col + 84]).then_inc(sem, 16)
+
+    if in_ag:
+        g.dma_start(T.a1[:], T.x1[:]).then_inc(S.agld, 16)
+    load(g.sync, others[0], 0, S.ld1)
+    load(g.scalar, others[0], 1, S.ld1)
+    load(g.sync, others[1], 0, S.ld1)
+    load(g.scalar, others[1], 1, S.ld1)
+    load(g.sync, ci, 0, S.ld2)
+    load(g.scalar, ci, 1, S.ld2)
+    sent = 0
+    stored = 0
+
+    tr = []
+    for kk in range(8):
+        if kk == k:
+            continue
+        c, h, q2 = role(kk)
+        tr.append(RemoteDMATransfer(dst_ids=[did(ci, kk)], dma_engine_mask=0x3 << (2 * len(tr)), remote_sem=S.e1,
+                                    src=T.d[_piece(c, h, q2)], dst=T.r1[k]))
+    g.wait_ge(S.ld1, 64)
+    g.remote_dma_fused(tr, local_sem=S.snd)
+    sent += 14
+
+    if in_ag:
+        m = G1.index(rank)
+        peers = [j for j in range(len(G1)) if j != m]
+        ids = []
+        for j in peers:
+            rid, pid, _se = topo.addr(T.cores[G1[j]])
+            ids.append(DstId(rid=rid, pnc=pid))
+        g.wait_ge(S.agld, 16)
+        g.remote_dma_fused([RemoteDMATransfer(dst_ids=ids, dma_engine_mask=0xFF, remote_sem=S.aga,
+                                              srcs=[T.a1[:]], dsts=[T.agl[m]] * len(peers))], local_sem=S.snd)
+        sent += 8
+        g.scalar.dma_start(T.y1[:, 256 * m:256 * m + 256], T.x1[:]).then_inc(S.st, 16)
+        for q, j in zip((g.sync, g.scalar), peers):
+            q.wait_ge(S.aga, 16)
+            q.dma_start(T.y1[:, 256 * j:256 * j + 256], T.agl[j]).then_inc(S.st, 16)
+        stored += 48
+
+    tr = []
+    for h in range(2):
+        for q2 in range(2):
+            f = _finisher(h, q2)
+            if f == k:
+                continue
+            tr.append(RemoteDMATransfer(dst_ids=[did(ci, f)], dma_engine_mask=0xF << (4 * len(tr)), remote_sem=S.e2,
+                                        src=T.d[_piece(ci, h, q2)], dst=T.r2[k]))
+    g.wait_ge(S.ld2, 32)
+    g.remote_dma_fused(tr, local_sem=S.snd)
+    sent += 4 * len(tr)
+
+    c, h, q2 = role(k)
+    srcs = [T.d[_piece(c, h, q2)] if s == k else T.r1[s] for s in range(8)]
+    g.wait_ge(S.e1, 14)
+    g.remote_dma_fused([RemoteDMATransfer(dst_ids=[did(c, _finisher(h, q2))], dma_engine_mask=0xFF, remote_sem=S.f1,
+                                          srcs=srcs, dsts=[T.pr[ci]], alu_op=1)], local_sem=S.snd)
+    sent += 8
+
+    if k % 4 >= 2:
+        h, q2 = 1 - k // 4, k % 2
+        srcs = [T.d[_piece(ci, h, q2)] if s == k else T.r2[s] for s in range(8)] + [T.pr[c] for c in others]
+        g.wait_ge(S.e2, 28)
+        g.wait_ge(S.f1, 16)
+        g.remote_dma_fused([RemoteDMATransfer(dst_ids=[did(ci, 4 * h + i) for i in range(4)], dma_engine_mask=0xFFFF,
+                                              remote_sem=S.f2, srcs=srcs, dsts=[T.fin[q2]] * 4, alu_op=1)],
+                           local_sem=S.snd)
+        sent += 16
+
+    i = k % 4
+    g.sync.wait_ge(S.f2, 32)
+    g.sync.dma_start(T.y2[:], T.fin[:, (i // 2)::2, 21 * (i % 2):21 * (i % 2) + 21]).then_inc(S.st, 16)
+    stored += 16
+
+    g.wait_ge(S.snd, sent)
+    g.wait_ge(S.st, stored)

@@ -6,10 +6,13 @@ SCRATCH = {
     "r2": ("dram", [8, 128, 42], "float32"),
     "pr": ("dram", [3, 128, 42], "float32"),
     "fin": ("dram", [2, 128, 42], "float32"),
-    "a1": ("dram", [128, 256], "bfloat16"),
-    "agl": ("dram", [3, 128, 256], "bfloat16"),
+    "a1": ("dram", [4, 128, 64], "bfloat16"),
+    "aq": ("dram", [128, 64], "bfloat16"),
+    "agl": ("dram", [12, 128, 64], "bfloat16"),
 }
-SEMAPHORES = ["ld1", "ld2", "e1", "e2", "f1", "f2", "snd", "st", "agld", "aga"]
+SEMAPHORES = ["ld1", "ld2", "e1", "e2", "f1", "f2", "snd", "st", "agld", "ags", "aga", "go"]
+
+RELAYS = (0, 1, 4, 5)
 
 
 def _piece(c, h, q2):
@@ -27,8 +30,7 @@ def rank_program(g, core, T, topo):
     S = T.sem
     ci, k = divmod(rank, 8)
     others = [c for c in range(3) if c != ci]
-    G1 = T.tables["G1"]
-    in_ag = rank in G1
+    in_ag = k == 0
 
     def did(c, kk):
         rid, pid, _se = topo.addr(T.cores[8 * c + kk])
@@ -42,12 +44,12 @@ def rank_program(g, core, T, topo):
         col = 168 * c + 84 * h
         q.dma_start(T.d[p:p + 2], T.x2[:, col:col + 84]).then_inc(sem, 16)
 
-    if in_ag:
-        g.dma_start(T.a1[:], T.x1[:]).then_inc(S.agld, 16)
     load(g.sync, others[0], 0, S.ld1)
     load(g.scalar, others[0], 1, S.ld1)
     load(g.sync, others[1], 0, S.ld1)
     load(g.scalar, others[1], 1, S.ld1)
+    if in_ag:
+        g.sync.dma_start(T.a1[:], T.x1[:]).then_inc(S.agld, 16)
     load(g.sync, ci, 0, S.ld2)
     load(g.scalar, ci, 1, S.ld2)
     sent = 0
@@ -65,45 +67,53 @@ def rank_program(g, core, T, topo):
     sent += 14
 
     if in_ag:
-        m = G1.index(rank)
-        peers = [j for j in range(len(G1)) if j != m]
-        ids = []
-        for j in peers:
-            rid, pid, _se = topo.addr(T.cores[G1[j]])
-            ids.append(DstId(rid=rid, pnc=pid))
         g.wait_ge(S.agld, 16)
-        g.remote_dma_fused([RemoteDMATransfer(dst_ids=ids, dma_engine_mask=0xFF, remote_sem=S.aga,
-                                              srcs=[T.a1[:]], dsts=[T.agl[m]] * len(peers))], local_sem=S.snd)
-        sent += 8
-        g.scalar.dma_start(T.y1[:, 256 * m:256 * m + 256], T.x1[:]).then_inc(S.st, 16)
-        for q, j in zip((g.sync, g.scalar), peers):
-            q.wait_ge(S.aga, 16)
-            q.dma_start(T.y1[:, 256 * j:256 * j + 256], T.agl[j]).then_inc(S.st, 16)
-        stored += 48
+        g.remote_dma_fused([RemoteDMATransfer(dst_ids=[did(ci, RELAYS[t])], dma_engine_mask=0xF << (4 * t),
+                                              remote_sem=S.ags, src=T.a1[t], dst=T.aq[:]) for t in (1, 2, 3)],
+                           local_sem=S.snd)
+        sent += 12
 
-    tr = []
+    c, h, q2 = role(k)
+    srcs = [T.d[_piece(c, h, q2)] if s == k else T.r1[s] for s in range(8)]
+    tr = [RemoteDMATransfer(dst_ids=[did(c, _finisher(h, q2))], dma_engine_mask=0xFF, remote_sem=S.f1,
+                            srcs=srcs, dsts=[T.pr[ci]], alu_op=1)]
+    sent += 8
     for h in range(2):
         for q2 in range(2):
             f = _finisher(h, q2)
             if f == k:
                 continue
-            tr.append(RemoteDMATransfer(dst_ids=[did(ci, f)], dma_engine_mask=0xF << (4 * len(tr)), remote_sem=S.e2,
-                                        src=T.d[_piece(ci, h, q2)], dst=T.r2[k]))
+            tr.append(RemoteDMATransfer(dst_ids=[did(ci, f)], dma_engine_mask=0x3 << (6 + 2 * len(tr)),
+                                        remote_sem=S.e2, src=T.d[_piece(ci, h, q2)], dst=T.r2[k]))
+            sent += 2
     g.wait_ge(S.ld2, 32)
-    g.remote_dma_fused(tr, local_sem=S.snd)
-    sent += 4 * len(tr)
-
-    c, h, q2 = role(k)
-    srcs = [T.d[_piece(c, h, q2)] if s == k else T.r1[s] for s in range(8)]
     g.wait_ge(S.e1, 14)
-    g.remote_dma_fused([RemoteDMATransfer(dst_ids=[did(c, _finisher(h, q2))], dma_engine_mask=0xFF, remote_sem=S.f1,
-                                          srcs=srcs, dsts=[T.pr[ci]], alu_op=1)], local_sem=S.snd)
-    sent += 8
+    g.remote_dma_fused(tr, local_sem=S.snd)
+
+    if k in RELAYS:
+        t = RELAYS.index(k)
+        if in_ag:
+            g.sem_inc(S.go, 1)
+            src = T.a1[0]
+        else:
+            g.wait_ge(S.ags, 4)
+            src = T.aq[:]
+        g.remote_dma_fused([RemoteDMATransfer(dst_ids=[did(c, 0) for c in others], dma_engine_mask=0xFF,
+                                              remote_sem=S.aga, srcs=[src], dsts=[T.agl[4 * ci + t]] * 2)],
+                           local_sem=S.snd)
+        sent += 8
+    if in_ag:
+        g.scalar.wait_ge(S.go, 1)
+        g.scalar.dma_start(T.y1[:, 256 * ci:256 * ci + 256], T.x1[:]).then_inc(S.st, 16)
+        g.scalar.wait_ge(S.aga, 64)
+        for j in others:
+            g.scalar.dma_start(T.y1[:, 256 * j:256 * j + 256], T.agl[4 * j:4 * j + 4]).then_inc(S.st, 16)
+        stored += 48
 
     if k % 4 >= 2:
         h, q2 = 1 - k // 4, k % 2
         srcs = [T.d[_piece(ci, h, q2)] if s == k else T.r2[s] for s in range(8)] + [T.pr[c] for c in others]
-        g.wait_ge(S.e2, 28)
+        g.wait_ge(S.e2, 14)
         g.wait_ge(S.f1, 16)
         g.remote_dma_fused([RemoteDMATransfer(dst_ids=[did(ci, 4 * h + i) for i in range(4)], dma_engine_mask=0xFFFF,
                                               remote_sem=S.f2, srcs=srcs, dsts=[T.fin[q2]] * 4, alu_op=1)],

@@ -10,7 +10,7 @@ SCRATCH = {
     "aq": ("dram", [128, 64], "bfloat16"),
     "agl": ("dram", [12, 128, 64], "bfloat16"),
 }
-SEMAPHORES = ["ld1", "ld2", "e1", "e2", "f1", "f2", "snd", "st", "agld", "ags", "aga", "go"]
+SEMAPHORES = ["lda", "ldb", "ld2", "e1", "e2", "f1", "f2", "snd", "st", "agld", "ags", "aga", "go"]
 
 RELAYS = (0, 1, 4, 5)
 
@@ -44,10 +44,10 @@ def rank_program(g, core, T, topo):
         col = 168 * c + 84 * h
         q.dma_start(T.d[p:p + 2], T.x2[:, col:col + 84]).then_inc(sem, 16)
 
-    load(g.sync, others[0], 0, S.ld1)
-    load(g.scalar, others[0], 1, S.ld1)
-    load(g.sync, others[1], 0, S.ld1)
-    load(g.scalar, others[1], 1, S.ld1)
+    load(g.sync, others[0], 0, S.lda)
+    load(g.scalar, others[1], 0, S.lda)
+    load(g.sync, others[0], 1, S.ldb)
+    load(g.scalar, others[1], 1, S.ldb)
     if in_ag:
         g.sync.dma_start(T.a1[:], T.x1[:]).then_inc(S.agld, 16)
     load(g.sync, ci, 0, S.ld2)
@@ -55,16 +55,17 @@ def rank_program(g, core, T, topo):
     sent = 0
     stored = 0
 
-    tr = []
-    for kk in range(8):
-        if kk == k:
-            continue
-        c, h, q2 = role(kk)
-        tr.append(RemoteDMATransfer(dst_ids=[did(ci, kk)], dma_engine_mask=0x3 << (2 * len(tr)), remote_sem=S.e1,
-                                    src=T.d[_piece(c, h, q2)], dst=T.r1[k]))
-    g.wait_ge(S.ld1, 64)
-    g.remote_dma_fused(tr, local_sem=S.snd)
-    sent += 14
+    for sem, kks in ((S.lda, (4, 5, 6, 7)), (S.ldb, (0, 1, 2, 3))):
+        tr = []
+        for kk in kks:
+            if kk == k:
+                continue
+            c, h, q2 = role(kk)
+            tr.append(RemoteDMATransfer(dst_ids=[did(ci, kk)], dma_engine_mask=0xF << (4 * len(tr)), remote_sem=S.e1,
+                                        src=T.d[_piece(c, h, q2)], dst=T.r1[k]))
+        g.wait_ge(sem, 32)
+        g.remote_dma_fused(tr, local_sem=S.snd)
+        sent += 4 * len(tr)
 
     if in_ag:
         g.wait_ge(S.agld, 16)
@@ -87,7 +88,7 @@ def rank_program(g, core, T, topo):
                                         remote_sem=S.e2, src=T.d[_piece(ci, h, q2)], dst=T.r2[k]))
             sent += 2
     g.wait_ge(S.ld2, 32)
-    g.wait_ge(S.e1, 14)
+    g.wait_ge(S.e1, 28)
     g.remote_dma_fused(tr, local_sem=S.snd)
 
     if k in RELAYS:

from concourse.bass import DstId, RemoteDMATransfer

SCRATCH = {
    "d": ("dram", [12, 128, 42], "float32"),
    "r1": ("dram", [8, 128, 42], "float32"),
    "r2": ("dram", [8, 128, 42], "float32"),
    "pr": ("dram", [3, 128, 42], "float32"),
    "fin": ("dram", [2, 128, 42], "float32"),
    "a1": ("dram", [4, 128, 64], "bfloat16"),
    "aq": ("dram", [128, 64], "bfloat16"),
    "agl": ("dram", [12, 128, 64], "bfloat16"),
}
SEMAPHORES = ["lda", "ldb", "ld2", "e1", "e2", "f1", "f2", "snd", "st", "agld", "ags", "aga", "go"]

RELAYS = (0, 1, 4, 5)


def _piece(c, h, q2):
    return (c * 2 + h) * 2 + q2


def _finisher(h, q2):
    return 4 * (1 - h) + 2 + q2


def rank_program(g, core, T, topo):
    rank = T.rank_of(core)
    if rank is None:
        return
    S = T.sem
    ci, k = divmod(rank, 8)
    others = [c for c in range(3) if c != ci]
    in_ag = k == 0

    def did(c, kk):
        rid, pid, _se = topo.addr(T.cores[8 * c + kk])
        return DstId(rid=rid, pnc=pid)

    def role(kk):
        return others[(kk % 4) // 2], 1 - kk // 4, kk % 2

    def load(q, c, h, sem):
        p = _piece(c, h, 0)
        col = 168 * c + 84 * h
        q.dma_start(T.d[p:p + 2], T.x2[:, col:col + 84]).then_inc(sem, 16)

    load(g.sync, others[0], 0, S.lda)
    load(g.scalar, others[1], 0, S.lda)
    load(g.sync, others[0], 1, S.ldb)
    load(g.scalar, others[1], 1, S.ldb)
    if in_ag:
        g.sync.dma_start(T.a1[:], T.x1[:]).then_inc(S.agld, 16)
    load(g.sync, ci, 0, S.ld2)
    load(g.scalar, ci, 1, S.ld2)
    sent = 0
    stored = 0

    for sem, kks in ((S.lda, (4, 5, 6, 7)), (S.ldb, (0, 1, 2, 3))):
        tr = []
        for kk in kks:
            if kk == k:
                continue
            c, h, q2 = role(kk)
            tr.append(RemoteDMATransfer(dst_ids=[did(ci, kk)], dma_engine_mask=0xF << (4 * len(tr)), remote_sem=S.e1,
                                        src=T.d[_piece(c, h, q2)], dst=T.r1[k]))
        g.wait_ge(sem, 32)
        g.remote_dma_fused(tr, local_sem=S.snd)
        sent += 4 * len(tr)

    if in_ag:
        g.wait_ge(S.agld, 16)
        g.remote_dma_fused([RemoteDMATransfer(dst_ids=[did(ci, RELAYS[t])], dma_engine_mask=0xF << (4 * t),
                                              remote_sem=S.ags, src=T.a1[t], dst=T.aq[:]) for t in (1, 2, 3)],
                           local_sem=S.snd)
        sent += 12

    c, h, q2 = role(k)
    srcs = [T.d[_piece(c, h, q2)] if s == k else T.r1[s] for s in range(8)]
    tr = [RemoteDMATransfer(dst_ids=[did(c, _finisher(h, q2))], dma_engine_mask=0xFF, remote_sem=S.f1,
                            srcs=srcs, dsts=[T.pr[ci]], alu_op=1)]
    sent += 8
    for h in range(2):
        for q2 in range(2):
            f = _finisher(h, q2)
            if f == k:
                continue
            tr.append(RemoteDMATransfer(dst_ids=[did(ci, f)], dma_engine_mask=0x3 << (6 + 2 * len(tr)),
                                        remote_sem=S.e2, src=T.d[_piece(ci, h, q2)], dst=T.r2[k]))
            sent += 2
    g.wait_ge(S.ld2, 32)
    g.wait_ge(S.e1, 28)
    g.remote_dma_fused(tr, local_sem=S.snd)

    if k in RELAYS:
        t = RELAYS.index(k)
        if in_ag:
            g.sem_inc(S.go, 1)
            src = T.a1[0]
        else:
            g.wait_ge(S.ags, 4)
            src = T.aq[:]
        g.remote_dma_fused([RemoteDMATransfer(dst_ids=[did(c, 0) for c in others], dma_engine_mask=0xFF,
                                              remote_sem=S.aga, srcs=[src], dsts=[T.agl[4 * ci + t]] * 2)],
                           local_sem=S.snd)
        sent += 8
    if in_ag:
        g.scalar.wait_ge(S.go, 1)
        g.scalar.dma_start(T.y1[:, 256 * ci:256 * ci + 256], T.x1[:]).then_inc(S.st, 16)
        g.scalar.wait_ge(S.aga, 64)
        for j in others:
            g.scalar.dma_start(T.y1[:, 256 * j:256 * j + 256], T.agl[4 * j:4 * j + 4]).then_inc(S.st, 16)
        stored += 48

    if k % 4 >= 2:
        h, q2 = 1 - k // 4, k % 2
        srcs = [T.d[_piece(ci, h, q2)] if s == k else T.r2[s] for s in range(8)] + [T.pr[c] for c in others]
        g.wait_ge(S.e2, 14)
        g.wait_ge(S.f1, 16)
        g.remote_dma_fused([RemoteDMATransfer(dst_ids=[did(ci, 4 * h + i) for i in range(4)], dma_engine_mask=0xFFFF,
                                              remote_sem=S.f2, srcs=srcs, dsts=[T.fin[q2]] * 4, alu_op=1)],
                           local_sem=S.snd)
        sent += 16

    i = k % 4
    g.sync.wait_ge(S.f2, 32)
    g.sync.dma_start(T.y2[:], T.fin[:, (i // 2)::2, 21 * (i % 2):21 * (i % 2) + 21]).then_inc(S.st, 16)
    stored += 16

    g.wait_ge(S.snd, sent)
    g.wait_ge(S.st, stored)
